import numpy as np
import ml_dtypes


def mxq(x, axis, fmt="e4m3"):
    dtype, down = {"e4m3": (ml_dtypes.float8_e4m3fn, 7), "e5m2": (ml_dtypes.float8_e5m2, 14)}[fmt]
    v = np.moveaxis(np.asarray(x, np.float32).astype(ml_dtypes.bfloat16).astype(np.float64), axis, -1)
    blocks = v.reshape(v.shape[:-1] + (-1, 32))
    amax = np.abs(blocks).max(-1, keepdims=True)
    byte = np.maximum(np.where(amax > 0, np.frexp(amax)[1] - 1 + 127, 0) - down, 1)
    scale = np.exp2(byte - 127.0)
    codes = (blocks / scale).astype(np.float32).astype(dtype).astype(np.float64)
    return np.moveaxis((codes * scale).reshape(v.shape), -1, axis)


WIDE = False


def mx_kscale(k):
    if not WIDE:
        return np.ones(k)
    levels = np.array([10, -10, 5, -5, 0])
    if k % 512:
        return np.exp2(np.random.permutation(np.resize(levels, k // 32))).repeat(32)
    a = np.empty((k // 512, 16))
    for p in range(k // 512):
        a[p, :8] = np.random.permutation(np.resize(levels, 8))
        for g in range(8):
            far = levels[np.abs(levels - a[p, g]) >= 10]
            a[p, g + 8] = far[np.random.randint(len(far))]
    return np.exp2(a.ravel()).repeat(32)


BF16 = ml_dtypes.bfloat16


def bf(x):
    return np.asarray(x, np.float32).astype(BF16)


def f64(x):
    return np.asarray(x).astype(np.float64)

def planes(Y):
    n, m = Y.shape
    b = f64(bf(Y)).reshape(n // 32, 32, m)
    amax = np.abs(b).max(1)
    byte = np.clip(np.where(amax > 0, np.frexp(amax)[1] - 1 + 127 - 7, 1), 1, 254)
    codes = (b * np.exp2(127.0 - byte)[:, None, :]).reshape(n, m).astype(np.float32).astype(ml_dtypes.float8_e4m3fn).view(np.uint8)
    words = codes.reshape(n // 512, 128, 4, m).transpose(0, 1, 3, 2)
    return np.ascontiguousarray(words), np.ascontiguousarray(byte.astype(np.uint8).reshape(n // 512, 16, m))


N, Q, G, P, C = 2048, 1024, 2, 512, 512


def soft_codes(x, key, nrm):
    l = (mxq(x, 2, "e4m3") @ mxq(key, 2, "e4m3").transpose(0, 2, 1)) - nrm[:, None, :]
    w = np.exp(l - l.max(-1, keepdims=True))
    return w / w.sum(-1, keepdims=True)


def merge_codes(t):
    g, r, c = t.shape
    return np.transpose(t, (1, 0, 2)).reshape(r, g * c)


def setup_inputs():
    s, u = mx_kscale(P), mx_kscale(P)
    t = mx_kscale(G * C).reshape(G, C)
    return {
        "x": bf(np.random.standard_normal((G, N, P)) * s),
        "q": bf(np.random.standard_normal((G, Q, P)) * u),
        "key": bf(np.random.standard_normal((G, C, P)) / np.sqrt(P) / s),
        "val": bf(np.random.standard_normal((G, C, P)) / np.sqrt(P) / u / t[:, :, None]),
        "nrm": bf(0.7 * np.random.standard_normal((G, C))),
        "gain": bf((1.0 + 0.1 * np.random.standard_normal((G, C))) * t),
        "base": bf(0.5 * np.random.standard_normal(Q)),
    }


def core(x, q, key, val, nrm, gain, base):
    num_codes = key.shape[1]
    a = soft_codes(f64(x), f64(key), f64(nrm))
    e = (num_codes * a - 1.0) * f64(gain)[:, None, :]
    lut = mxq(f64(q), 2, "e4m3") @ mxq(f64(val), 2, "e4m3").transpose(0, 2, 1)
    e_flat = merge_codes(e)
    lut_flat = merge_codes(lut)
    s = mxq(e_flat, 1, "e4m3") @ mxq(lut_flat, 1, "e4m3").T
    k_scale = np.sqrt(e_flat.shape[1])
    return s / k_scale + f64(base)[None, :]


def reference(x, q, key, val, nrm, gain, base):
    R_out = core(x, q, key, val, nrm, gain, base)
    words, scales = planes(R_out.T)
    return R_out, words, scales

@@ -1,0 +1,377 @@
+from contextlib import ExitStack
+
+import concourse.mybir as mybir
+from concourse.masks import make_identity
+
+N, Q, G, D, C = 2048, 1024, 2, 512, 512
+FLOPS = 2 * G * N * D * C + 2 * G * Q * D * C + 2 * N * Q * G * C
+
+F32 = mybir.dt.float32
+BF16 = mybir.dt.bfloat16
+U32 = mybir.dt.uint32
+I32 = mybir.dt.int32
+U8 = mybir.dt.uint8
+FP8X4 = mybir.dt.float8_e4m3fn_x4
+ALU = mybir.AluOpType
+ACT = mybir.ActivationFunctionType
+
+P = 128
+PAIR = 256
+UNITS = 16
+WARM = 0
+ORDER = """
+nt0 kt0 nc0:S kt1 kc0:S kq0 xt0 kc1:S kq1 xt1 xc0:S kt3 xc1:S xq0 kc3:V kt2
+L0 kc2:S xq1 L1 kq3 nt1 T0 kt4 nc1:S kq2 xt2 M0 kc4:S kt5 T1 X0
+L2 kq4 kc5:S M1 kt6 T2 X1 L3 kq5 kt9 xc2:S R0 T3 kt7 N1:G kc6:S
+M2 kt8 N0:G kc7:S M3 et1 kc8:S et0 bc xq2 kt12 kq7 X3 kq6 kt10 eg0
+X2 eg1 lm0 kc10:S L4 R1 L5 kq8 lc0:S N3:G T4 xt3 kc9:S T5 N2:G lm1
+xc3:S M4 kt11 lc1:S eq0 xt4 kc11:V kc12:S lm2 xq3 lm3 xc4:S M5 et2 lc2:S kq9
+et3 kq10 kt14 lc3:S kq12 kq11 X5 lm4 eg3 lm7 lc4:S lq1 lm5 eg2 L6 L7
+lc5:S xq4 lm6 eq1 X4 kt13 lq2 lq0 lc6:S kt15 R2 T6 N4:G kc13:S lm8 T7
+N5:G kc14:S xt5 M6 et4 lc7:S kq13 et5 kq14 kc15:S lm9 M7 lm11 X6 lm10 kq15
+L8 lq3 lc11:S eg4 lc8:S L9 eg5 S0 lc9:S T8 F0:V lm12 X7 S1 xc5:S lm13
+eq2 lq4 lc10:S xt6 xq5 R3 T9 lc12:S lm14 N6:G lm15 M8 F1:S N7:G bt1 M9
+lc13:S et6 I1:G lc15:V et7 X8 bt0 eg6 I0:G X9 L10 eg7 L11 xc6:S xt7 lq6
+lc14:S lq5 S2 eq3 bk0:S xq6 S4 R4 lq7 bk1:S sr0 N8:G T10 S3 F2:S sr1
+T11 N9:G L12 F3:S M10 et8 et9 M11 I2:G X10 bt2 bt3 eg9 bk2:S I3:G L13
+eg8 X11 xt8 sr2 oq0 eq4 xc7:S S5 R5 sw0 T12 N10:G F4:S S7 T13 S6
+N11:G F5:S M12 bk3:S et10 I4:G M13 et11 X12 sr3 bt4 eg10 I5:G bk4:V bt5 X13
+xt9 xc8:S xt10 xq7 sr4 eg11 bk5:S xt11 xq8 F6:S sr5 oq1 L14 eq5 L15 xc9:S
+L16 R6 sw1 T14 N12:G L17 F7:S T15 bt6 N13:G xc10:S M14 et12 I6:G et13 M15
+X14 bt7 eg12 I7:G X15 S8 eg13 bk6:S S9 oq2 bk7:S S10 eq6 sr6 R7 sw2
+xq9 F8:S S11 sr7 N14:G T16 L18 F9:S T17 N15:G bt8 F10:S M16 et14 I8:G et15
+M17 X16 bt9 I9:G eg14 X17 L19 eg15 bk8:S xt12 oq3 bk9:S xt13 eq7 sr8 xq10
+sw3 F11:S bt10 R8 sr9 T18 N16:G xc11:S T19 bt11 N17:G et16 bk10:S M18 L20 I11:G
+M19 sr10 X18 et17 eg16 L21 I10:G X19 S12 eg17 bk11:S S13 oq4 F12:S eq8 S14
+sr11 xq11 sw4 F13:S R9 T20 bt12 N18:G xc12:S T21 bt13 N19:G et18 bk12:S M20 L22
+I12:G M21 sr12 X20 et19 eg18 I13:G S15 X21 eg19 L23 F14:S xt14 R10 oq5 F15:S
+N20:G T22 bt14 sw5 xc13:S T23 N21:G et20 bk14:S M22 bt15 I14:G et21 M23 sr14 X22
+xt15 I15:G eg20 X23 eg21 bk15:S eq9 S16 bk13:S xq12 sr15 oq6 xc14:S eq10 sr13 L24
+xq13 sw6 L25 F16:S R11 S17 T24 N22:G xc15:S L27 T25 N23:G L26 F17:S M24 et22
+et23 M25 I16:G X24 bt16 eg22 bt17 X25 I17:G eg23 S18 bk17:S S19 oq7 F18:S eq11
+sr17 S21 xq14 sw7 F19:S R12 T26 N24:G bk16:S bt18 T27 N25:G et24 bk18:S M26 sr16
+bt19 I18:G et25 M27 X26 sr18 L29 eg24 I19:G X27 L28 S20 eg25 bk19:S S22 oq8
+F20:S eq12 sr19 S23 xq15 sw8 F21:S R13 T28 N27:G bt20 F22:S T29 bt21 N26:G et27
+bk20:S M28 I20:G et26 M29 sr20 X28 L30 eg27 I21:G X29 L31 eg26 bk21:S oq9 F23:S
+bt22 eq13 sr21 R14 sw9 T30 N28:G bt23 T31 bk22:S N29:G et28 M30 bk23:S sr22 I22:G
+et29 M31 X30 sr23 S25 eg28 I23:G X31 S24 eg29 F25:S S27 oq10 F24:S eq14 S26
+R15 sw10 oq11 F27:S N30:G F26:V bt24 ss0 bt25 sw11 N31:G bk24:S et30 bk25:V bt26 I24:G
+sr24 et31 eg30 bk26:S sr25 bt27 I25:G eg31 sr26 bk27:S I26:G sr27 I27:G eq15 S28 oq12
+oq13 sw12 S29 sw13 F28:S S30 F29:S bt28 F30:S I29:G bt29 bk28:V S31 bk29:S I28:G sr28
+F31:S bt31 sr29 oq14 I31:V bt30 sw14 I30:G bk31:S bk30:S sr31 oq15 sr30 ss1 sw15
+"""
+LOADS = "k0a x0 k0b k1 x1 v0 q00 x2 v1 q10 x3 q01 q11 c"
+
+
+def tile_softproductquantasymmetricscores_x1_kernel(tc, x, q, key, val, nrm, gain, base, out_0, out_1, out_2):
+    nc = tc.nc
+    with ExitStack() as ctx:
+        keep = ctx.enter_context(tc.tile_pool(name="keep", bufs=1))
+        work = ctx.enter_context(tc.tile_pool(name="work", bufs=3))
+        psum = ctx.enter_context(tc.psum_pool(name="psum", bufs=1))
+        ctx.enter_context(tc.manual_schedule())
+
+        free_banks = list(range(8))
+        held = {}
+
+        def bank(name, shape):
+            n = free_banks[0]
+            free_banks.remove(n)
+            held[name] = n
+            return psum.tile(shape, F32, name="bank%d" % n, tag="bank%d" % n)
+
+        def release(name):
+            free_banks.append(held[name])
+
+        key_sb = [keep.tile([P, 4, D], BF16, name="key_sb%d" % g) for g in range(G)]
+        val_sb = [keep.tile([P, 4, D], BF16, name="val_sb%d" % g) for g in range(G)]
+        q_sb = [[keep.tile([P, 4, D], BF16, name="q_sb%d%d" % (g, h)) for h in range(2)] for g in range(G)]
+        x_sb = [keep.tile([P, 2, D], BF16, name="x_sb%d" % u) for u in range(UNITS)]
+        nrm_col = keep.tile([P, G, 4], BF16, name="nrm_col")
+        gain_col = keep.tile([P, G, 4], BF16, name="gain_col")
+        base_col = keep.tile([P, 2, 4], BF16, name="base_col")
+
+        def load_book(dst, rows):
+            nc.sync.dma_start(out=dst, in_=rows.rearrange("(m t) k -> m t k", t=4))
+
+        def load_x(u):
+            j, g = divmod(u, G)
+            nc.sync.dma_start(out=x_sb[u][:], in_=x[g, PAIR * j : PAIR * (j + 1), :].rearrange("(a p) k -> p a k", a=2))
+
+        key0 = key[0].rearrange("(m t) k -> m t k", t=4)
+        nc.scalar.dma_start(out=nrm_col[:], in_=nrm.rearrange("g (m t) -> m g t", t=4))
+        done = []
+        for w in LOADS.split():
+            if w == "k0a":
+                nc.sync.dma_start(out=key_sb[0][:, 0:2, :], in_=key0[:, 0:2, :])
+            elif w == "k0b":
+                nc.sync.dma_start(out=key_sb[0][:, 2:4, :], in_=key0[:, 2:4, :])
+            elif w == "k1":
+                load_book(key_sb[1][:], key[1])
+            elif w == "c":
+                nc.sync.dma_start(out=gain_col[:], in_=gain.rearrange("g (m t) -> m g t", t=4))
+                nc.sync.dma_start(out=base_col[:], in_=base.rearrange("(h m t) -> m h t", h=2, t=4))
+            elif w[0] == "x":
+                load_x(len(done))
+                done.append(w)
+            elif w[0] == "v":
+                load_book(val_sb[int(w[1])][:], val[int(w[1])])
+            else:
+                load_book(q_sb[int(w[1])][int(w[2])][:], q[int(w[1]), 512 * int(w[2]) : 512 * (int(w[2]) + 1), :])
+        for u in range(len(done), UNITS):
+            load_x(u)
+
+        ident = keep.tile([P, P], F32, name="ident")
+        make_identity(nc, ident[:])
+        ident_bf = keep.tile([P, P], BF16, name="ident_bf")
+        nc.vector.tensor_copy(out=ident_bf[:], in_=ident[:])
+        warm = keep.tile([P, 1], F32, name="warm")
+        nc.scalar.activation(out=warm[:], in_=ident[:, 0:1], func=ACT.Exp)
+
+        nrm_bc = keep.tile([P, G, C], F32, name="nrm_bc")
+        base_f = keep.tile([P, 2, 4], F32, name="base_f")
+
+        def mx_tiles(name, width):
+            return (keep.tile([P, width], U32, name=name + "_codes", align_bytes=64),
+                    keep.tile([P, width], U8, name=name + "_scales", align_bytes=64))
+
+        key_mx = [mx_tiles("key%d" % g, C) for g in range(G)]
+        val_mx = [mx_tiles("val%d" % g, C) for g in range(G)]
+        q_mx = [mx_tiles("q%d" % g, Q) for g in range(G)]
+        lut_mx = [mx_tiles("lut%d" % g, Q) for g in range(G)]
+        x_mx = {}
+        e_mx = [mx_tiles("e%d" % u, PAIR) for u in range(UNITS)]
+        out_codes = keep.tile([P, 2, N], U32, name="out_codes", align_bytes=64)
+        out_scales = keep.tile([P, 2, N], U8, name="out_scales", align_bytes=64)
+
+        def quantise(codes, scales, grouped):
+            nc.vector.quantize_mx(out=codes.bitcast(FP8X4), scales=scales, in_=grouped[:].rearrange("p n t -> p (n t)"))
+
+        def mx(out, lhs, lcols, rhs, rcols, start, stop):
+            nc.tensor.matmul_mx(out=out, lhsT=lhs[0][:, lcols].bitcast(FP8X4), lhsT_scale=lhs[1][:, lcols],
+                                rhs=rhs[0][:, rcols].bitcast(FP8X4), rhs_scale=rhs[1][:, rcols], start=start, stop=stop)
+
+        st = {}
+        tasks = {}
+
+        def evac(dst, src, eng):
+            if eng == "V":
+                nc.vector.tensor_copy(out=dst, in_=src)
+            else:
+                nc.scalar.copy(out=dst, in_=src)
+
+        def shared(name, tag, shape, dtype, bufs):
+            if name not in st:
+                st[name] = work.tile(shape, dtype, name=tag, tag=tag, bufs=bufs, align_bytes=64)
+            return st[name]
+
+        def grouped(name):
+            return shared(("grp", name), "grouped", [P, PAIR, 4], BF16, 10)
+
+        def turn(eng, name, src):
+            turned = bank(name, [P, 2, 2, P])
+            st[name] = turned
+            for a in range(2):
+                words = src[:, a, :].bitcast(F32)
+                for u in range(2):
+                    nc.tensor.transpose(turned[:, a, u, :], words[:, u : D // 2 : 2], ident[:])
+
+        def regroup(eng, name):
+            dst = grouped(name)[:].rearrange("p n t -> p (n t)").bitcast(F32).rearrange("p (a r u) -> p a r u", a=2, u=2)
+            evac(dst, st[name][:].rearrange("p a u r -> p a r u"), eng)
+            release(name)
+
+        def quant(eng, name, codes, scales):
+            quantise(codes, scales, grouped(name))
+
+        def quant_x(eng, u):
+            x_codes = work.tile([P, PAIR], U32, name="x_codes", align_bytes=64, bufs=4)
+            x_scales = work.tile([P, PAIR], U8, name="x_scales", align_bytes=64, bufs=4)
+            x_mx[u] = (x_codes, x_scales)
+            quantise(x_codes[:], x_scales[:], grouped(("x", u)))
+
+        def warm_up(eng):
+            wb = bank("warm", [P, C])
+            for i in range(WARM):
+                nc.tensor.matmul(wb[:], lhsT=ident_bf[:], rhs=zeros[:], start=True, stop=True)
+            release("warm")
+
+        def nrm_spread(eng, g):
+            nb = bank(("nb", g), [P, 4, P])
+            st["nb", g] = nb
+            for t in range(4):
+                nc.tensor.matmul(nb[:, t, :], lhsT=nrm_col[:, g, t : t + 1].to_broadcast([P, P]), rhs=ident_bf[:], start=True, stop=True)
+
+        def nrm_copy(eng, g):
+            evac(nrm_bc[:, g, :], st["nb", g][:].rearrange("p t n -> p (t n)"), eng)
+            release(("nb", g))
+
+        def base_cast(eng):
+            nc.vector.tensor_copy(out=base_f[:], in_=base_col[:])
+
+        def lut_matmuls(eng, g, col):
+            lb = bank(("lut", g, col), [P, 4, P])
+            st["lut", g, col] = lb
+            for t in range(4):
+                mx(lb[:, t, :], val_mx[g], slice(P * t, P * (t + 1)), q_mx[g], slice(col, col + P), True, True)
+
+        def lut_copy(eng, g, col):
+            off = col % PAIR
+            evac(grouped(("lut", g, col - off))[:, off : off + P, :], st["lut", g, col][:].rearrange("p t n -> p n t"), eng)
+            release(("lut", g, col))
+
+        def logits(eng, u, a):
+            lb = bank(("l", u, a), [P, C])
+            st["l", u, a] = lb
+            mx(lb[:], x_mx[u], slice(P * a, P * (a + 1)), key_mx[u % G], slice(0, C), True, True)
+
+        def offsets(eng, u, a):
+            neg = shared(("neg", u), "neg", [P, 2, C], F32, 3)
+            nc.vector.tensor_tensor(out=neg[:, a, :], in0=nrm_bc[:, u % G, :], in1=st["l", u, a][:], op=ALU.subtract)
+            release(("l", u, a))
+
+        def minimum(eng, u, a):
+            mn = shared(("mn", u), "mn", [P, 2], F32, 4)
+            nc.vector.tensor_reduce(out=mn[:, a : a + 1], in_=st["neg", u][:, a, :], axis=mybir.AxisListType.X, op=ALU.min)
+
+        def expo(eng, u, a):
+            w = shared(("w", u), "w", [P, 2, C], F32, 3)
+            sm = shared(("sm", u), "sm", [P, 2], F32, 4)
+            nc.scalar.activation(out=w[:, a, :], in_=st["neg", u][:, a, :], func=ACT.Exp, scale=-1.0, bias=st["mn", u][:, a : a + 1],
+                                 accum_out=sm[:, a : a + 1])
+
+        def recip(eng, u):
+            rc = shared(("rc", u), "rc", [P, 2], F32, 4)
+            nc.vector.reciprocal(out=rc[:], in_=st["sm", u][:])
+
+        def normalise(eng, u, a):
+            un = shared(("un", u, a), "un", [P, C], F32, 4)
+            e = nc.vector if eng == "V" else nc.gpsimd
+            e.tensor_scalar(out=un[:], in0=st["w", u][:, a, :], scalar1=st["rc", u][:, a : a + 1], scalar2=float(C), op0=ALU.mult, op1=ALU.mult)
+
+        def e_turn(eng, u, a):
+            eb = bank(("et", u, a), [P, 4, P])
+            st["et", u, a] = eb
+            for t in range(4):
+                nc.tensor.transpose(eb[:, t, :], st["un", u, a][:, P * t : P * (t + 1)], ident[:])
+
+        def e_gain(eng, u, a):
+            nc.vector.scalar_tensor_tensor(
+                out=grouped(("e", u))[:, P * a : P * (a + 1), :], in0=st["et", u, a][:].rearrange("p t n -> p n t"), scalar=1.0,
+                in1=gain_col[:, u % G, :].unsqueeze(1).to_broadcast([P, P, 4]), op0=ALU.subtract, op1=ALU.mult)
+            release(("et", u, a))
+
+        def scores(eng, v, b):
+            j, h = divmod(v, 2)
+            sb = bank(("s", v, b), [P, 2, PAIR])
+            st["s", v, b] = sb
+            for tt in range(2):
+                t = 2 * b + tt
+                for g in range(G):
+                    mx(sb[:, tt, :], lut_mx[g], slice(512 * h + P * t, 512 * h + P * (t + 1)), e_mx[G * j + g], slice(0, PAIR), g == 0, g == G - 1)
+
+        def finish(eng, v, b):
+            h = v % 2
+            pf = shared(("pf", v), "pf", [P, 4, PAIR], F32, 3)
+            for t in (2 * b, 2 * b + 1):
+                src = st["s", v, b][:, t % 2, :]
+                if eng == "V":
+                    nc.vector.tensor_scalar(out=pf[:, t, :], in0=src, scalar1=1.0 / 32.0, scalar2=base_f[:, h, t : t + 1], op0=ALU.mult, op1=ALU.add)
+                else:
+                    nc.scalar.activation(out=pf[:, t, :], in_=src, func=ACT.Identity, scale=1.0 / 32.0, bias=base_f[:, h, t : t + 1])
+            release(("s", v, b))
+
+        def interleave(eng, v, a):
+            src = st["pf", v][:, :, P * a : P * (a + 1)].rearrange("p t n -> p n t")
+            dst = grouped(("o", v))[:, P * a : P * (a + 1), :]
+            if eng == "V":
+                nc.vector.tensor_copy(out=dst, in_=src)
+            else:
+                nc.gpsimd.tensor_scalar(out=dst, in0=src, scalar1=1.0, scalar2=1.0, op0=ALU.mult, op1=ALU.mult)
+
+        def store_words(eng, v):
+            j, h = divmod(v, 2)
+            cols = slice(PAIR * j, PAIR * (j + 1))
+            nc.sync.dma_start(out=out_1[h, :, cols, :].rearrange("p n t -> p (n t)").bitcast(I32), in_=out_codes[:, h, cols].bitcast(I32))
+
+        def store_scales(eng, part):
+            cols = slice(0, 1536) if part == 0 else slice(1536, N)
+            for quad in range(4):
+                nc.sync.dma_start(out=out_2[:, 4 * quad : 4 * quad + 4, cols].rearrange("h r n -> r h n").bitcast(I32),
+                                  in_=out_scales[32 * quad : 32 * quad + 4, :, cols].bitcast(I32))
+
+        def back_turn(eng, v, a):
+            bb = bank(("b", v, a), [P, 4, P])
+            st["b", v, a] = bb
+            for t in range(4):
+                nc.tensor.transpose(bb[:, t, :], st["pf", v][:, t, P * a : P * (a + 1)], ident[:])
+
+        def back_copy(eng, v, a):
+            res = shared(("res", v, a), "res", [P, 512], F32, 6)
+            evac(res[:].rearrange("r (m t) -> r m t", t=4), st["b", v, a][:].rearrange("r t m -> r m t"), eng)
+            release(("b", v, a))
+
+        def store_rows(eng, v, a):
+            j, h = divmod(v, 2)
+            rows = slice(PAIR * j + P * a, PAIR * j + P * (a + 1))
+            nc.sync.dma_start(out=out_0[rows, 512 * h : 512 * (h + 1)], in_=st["res", v, a][:])
+
+        def add(name, fn, *args):
+            tasks[name] = (fn, args)
+
+        if WARM:
+            zeros = keep.tile([P, C], BF16, name="zeros")
+            nc.vector.memset(zeros[:], 0.0)
+            add("W", warm_up)
+        for g in range(G):
+            add("nt%d" % g, nrm_spread, g)
+            add("nc%d" % g, nrm_copy, g)
+        add("bc", base_cast)
+        i = 0
+        for src, dst, col in ([(key_sb[0], key_mx[0], 0), (key_sb[1], key_mx[1], 0), (val_sb[0], val_mx[0], 0), (q_sb[0][0], q_mx[0], 0),
+                               (val_sb[1], val_mx[1], 0), (q_sb[1][0], q_mx[1], 0), (q_sb[0][1], q_mx[0], 512), (q_sb[1][1], q_mx[1], 512)]):
+            for hh in range(2):
+                cols = slice(col + PAIR * hh, col + PAIR * (hh + 1))
+                add("kt%d" % i, turn, ("book", i), src[:, 2 * hh : 2 * hh + 2, :])
+                add("kc%d" % i, regroup, ("book", i))
+                add("kq%d" % i, quant, ("book", i), dst[0][:, cols], dst[1][:, cols])
+                i += 1
+        for i, (g, col) in enumerate([(0, 0), (0, 256), (1, 0), (1, 256), (0, 512), (0, 768), (1, 512), (1, 768)]):
+            for b in range(2):
+                add("lm%d" % (2 * i + b), lut_matmuls, g, col + P * b)
+                add("lc%d" % (2 * i + b), lut_copy, g, col + P * b)
+            add("lq%d" % i, quant, ("lut", g, col), lut_mx[g][0][:, col : col + PAIR], lut_mx[g][1][:, col : col + PAIR])
+        for u in range(UNITS):
+            add("xt%d" % u, turn, ("x", u), x_sb[u])
+            add("xc%d" % u, regroup, ("x", u))
+            add("xq%d" % u, quant_x, u)
+            for a in range(2):
+                add("L%d" % (2 * u + a), logits, u, a)
+                add("T%d" % (2 * u + a), offsets, u, a)
+                add("M%d" % (2 * u + a), minimum, u, a)
+                add("X%d" % (2 * u + a), expo, u, a)
+            add("R%d" % u, recip, u)
+            for a in range(2):
+                add("N%d" % (2 * u + a), normalise, u, a)
+                add("et%d" % (2 * u + a), e_turn, u, a)
+                add("eg%d" % (2 * u + a), e_gain, u, a)
+            add("eq%d" % u, quant, ("e", u), e_mx[u][0][:], e_mx[u][1][:])
+        for v in range(UNITS):
+            j, h = divmod(v, 2)
+            cols = slice(PAIR * j, PAIR * (j + 1))
+            for b in range(2):
+                add("S%d" % (2 * v + b), scores, v, b)
+                add("F%d" % (2 * v + b), finish, v, b)
+            for a in range(2):
+                add("bt%d" % (2 * v + a), back_turn, v, a)
+                add("bk%d" % (2 * v + a), back_copy, v, a)
+                add("sr%d" % (2 * v + a), store_rows, v, a)
+            for a in range(2):
+                add("I%d" % (2 * v + a), interleave, v, a)
+            add("oq%d" % v, quant, ("o", v), out_codes[:, h, cols], out_scales[:, h, cols])
+            add("sw%d" % v, store_words, v)
+            if v in (11, 15):
+                add("ss%d" % (v // 12), store_scales, v // 12)
+        for word in ORDER.split() or list(tasks):
+            name, eng = (word + ":").split(":")[:2]
+            tasks[name][0](eng, *tasks[name][1])

@@ -18,47 +18,49 @@ ACT = mybir.ActivationFunctionType
 P = 128
 PAIR = 256
 UNITS = 16
-WARM = 0
+WARM = 6
+SPLIT = 192
 ORDER = """
-nt0 kt0 nc0:S kt1 kc0:S kq0 xt0 kc1:S kq1 xt1 xc0:S kt3 xc1:S xq0 kc3:V kt2
-L0 kc2:S xq1 L1 kq3 nt1 T0 kt4 nc1:S kq2 xt2 M0 kc4:S kt5 T1 X0
-L2 kq4 kc5:S M1 kt6 T2 X1 L3 kq5 kt9 xc2:S R0 T3 kt7 N1:G kc6:S
-M2 kt8 N0:G kc7:S M3 et1 kc8:S et0 bc xq2 kt12 kq7 X3 kq6 kt10 eg0
-X2 eg1 lm0 kc10:S L4 R1 L5 kq8 lc0:S N3:G T4 xt3 kc9:S T5 N2:G lm1
-xc3:S M4 kt11 lc1:S eq0 xt4 kc11:V kc12:S lm2 xq3 lm3 xc4:S M5 et2 lc2:S kq9
-et3 kq10 kt14 lc3:S kq12 kq11 X5 lm4 eg3 lm7 lc4:S lq1 lm5 eg2 L6 L7
-lc5:S xq4 lm6 eq1 X4 kt13 lq2 lq0 lc6:S kt15 R2 T6 N4:G kc13:S lm8 T7
-N5:G kc14:S xt5 M6 et4 lc7:S kq13 et5 kq14 kc15:S lm9 M7 lm11 X6 lm10 kq15
-L8 lq3 lc11:S eg4 lc8:S L9 eg5 S0 lc9:S T8 F0:V lm12 X7 S1 xc5:S lm13
-eq2 lq4 lc10:S xt6 xq5 R3 T9 lc12:S lm14 N6:G lm15 M8 F1:S N7:G bt1 M9
-lc13:S et6 I1:G lc15:V et7 X8 bt0 eg6 I0:G X9 L10 eg7 L11 xc6:S xt7 lq6
-lc14:S lq5 S2 eq3 bk0:S xq6 S4 R4 lq7 bk1:S sr0 N8:G T10 S3 F2:S sr1
-T11 N9:G L12 F3:S M10 et8 et9 M11 I2:G X10 bt2 bt3 eg9 bk2:S I3:G L13
-eg8 X11 xt8 sr2 oq0 eq4 xc7:S S5 R5 sw0 T12 N10:G F4:S S7 T13 S6
-N11:G F5:S M12 bk3:S et10 I4:G M13 et11 X12 sr3 bt4 eg10 I5:G bk4:V bt5 X13
-xt9 xc8:S xt10 xq7 sr4 eg11 bk5:S xt11 xq8 F6:S sr5 oq1 L14 eq5 L15 xc9:S
-L16 R6 sw1 T14 N12:G L17 F7:S T15 bt6 N13:G xc10:S M14 et12 I6:G et13 M15
-X14 bt7 eg12 I7:G X15 S8 eg13 bk6:S S9 oq2 bk7:S S10 eq6 sr6 R7 sw2
-xq9 F8:S S11 sr7 N14:G T16 L18 F9:S T17 N15:G bt8 F10:S M16 et14 I8:G et15
-M17 X16 bt9 I9:G eg14 X17 L19 eg15 bk8:S xt12 oq3 bk9:S xt13 eq7 sr8 xq10
-sw3 F11:S bt10 R8 sr9 T18 N16:G xc11:S T19 bt11 N17:G et16 bk10:S M18 L20 I11:G
-M19 sr10 X18 et17 eg16 L21 I10:G X19 S12 eg17 bk11:S S13 oq4 F12:S eq8 S14
-sr11 xq11 sw4 F13:S R9 T20 bt12 N18:G xc12:S T21 bt13 N19:G et18 bk12:S M20 L22
-I12:G M21 sr12 X20 et19 eg18 I13:G S15 X21 eg19 L23 F14:S xt14 R10 oq5 F15:S
-N20:G T22 bt14 sw5 xc13:S T23 N21:G et20 bk14:S M22 bt15 I14:G et21 M23 sr14 X22
-xt15 I15:G eg20 X23 eg21 bk15:S eq9 S16 bk13:S xq12 sr15 oq6 xc14:S eq10 sr13 L24
-xq13 sw6 L25 F16:S R11 S17 T24 N22:G xc15:S L27 T25 N23:G L26 F17:S M24 et22
-et23 M25 I16:G X24 bt16 eg22 bt17 X25 I17:G eg23 S18 bk17:S S19 oq7 F18:S eq11
-sr17 S21 xq14 sw7 F19:S R12 T26 N24:G bk16:S bt18 T27 N25:G et24 bk18:S M26 sr16
-bt19 I18:G et25 M27 X26 sr18 L29 eg24 I19:G X27 L28 S20 eg25 bk19:S S22 oq8
-F20:S eq12 sr19 S23 xq15 sw8 F21:S R13 T28 N27:G bt20 F22:S T29 bt21 N26:G et27
-bk20:S M28 I20:G et26 M29 sr20 X28 L30 eg27 I21:G X29 L31 eg26 bk21:S oq9 F23:S
-bt22 eq13 sr21 R14 sw9 T30 N28:G bt23 T31 bk22:S N29:G et28 M30 bk23:S sr22 I22:G
-et29 M31 X30 sr23 S25 eg28 I23:G X31 S24 eg29 F25:S S27 oq10 F24:S eq14 S26
-R15 sw10 oq11 F27:S N30:G F26:V bt24 ss0 bt25 sw11 N31:G bk24:S et30 bk25:V bt26 I24:G
-sr24 et31 eg30 bk26:S sr25 bt27 I25:G eg31 sr26 bk27:S I26:G sr27 I27:G eq15 S28 oq12
-oq13 sw12 S29 sw13 F28:S S30 F29:S bt28 F30:S I29:G bt29 bk28:V S31 bk29:S I28:G sr28
-F31:S bt31 sr29 oq14 I31:V bt30 sw14 I30:G bk31:S bk30:S sr31 oq15 sr30 ss1 sw15
+w1:W w2:W w4:W kt0:T w5:W nt1 xt0:T nt0 kt3:T w0:T w3:T kt1:T xt1:W kc1:S kc0:V kq0
+xc0:V xq0 kc3:V kq3 kq1 nc0:V kt4:T kc4:S kt2:W kc2:S xc1:S kq2 kq4 kt5:W kt6:T L1
+L0 kt7:T kt8:T kc5:S kc6:S kc7:S kt9:W xq1 T1 T0 M1 kq7 M0 kq6 kc8:V kq5
+xt2:W kt10:W kc9:S kq9 kq8 xc2:V X1 X0 kc10:S kq10 xq2 R0 nc1:S xt3:T kt11:W kc11:S
+xc3:S L3 L2 kt13:T kc13:S kt14:W kt12:W T3 T2 M3 N0:G N1:G et0 et1 xt4:T kt15:T
+xq3 M2 bc kq11 kq13 eg0 X3 X2 kc14:S kc12:S eg1 kq14 eq0 R1 kq12 L5
+xc4:S kc15:S lm1 L4 lm0 lc1:S lm4 lm2 N3:G N2:G L7 xt5:T et2 lc0:S lc2:S T5
+T4 M5 M4 kq15 xq4 eg2 lq0 X5 X4 R2 xc5:S lc4:S et3 eg3 lm7 L6
+T6 lc7:S T7 N5:G N4:G M6 lm10 lm6 lm3 lm5 lc6:S lc5:S lq3 M7 lq2 lm8
+lm14 lc3:S lc8:S lm9 et4 et5 lm15 eg4 lq1 eg5 eq1 X6 X7 R3 L9 L8
+xt6:T lc9:S lm11 lc14:S xc6:S lm13 lc10:S lc13:S lc15:S lc11:S xq5 T9 T8 N6:V eq2 M9
+M8 lq4 N7:G S1 X9 X8 et6 L11 lm12 et7 eg6 lq7 lq5 eg7 S0 L10
+lc12:S xq6 eq3 R4 lq6 F1:S F0:S L12 xt7:W N8:G T11 T10 M11 et8 eg8 M10
+N9:G bt0 et9 xc7:S X11 eg9 xq7 L13 S2 bk0:S X10 F2:S S3 F3:S I1:G I0:G
+oq0 eq4 sr0 bt1 sw0 bk1:S sr1 R5 T12 xt8:T xc8:S N10:G L14 bt2 T13 N11:G
+et10 bt3 et11 M12 M13 bk2:S X12 X13 eg10 eg11 S4 xq8 I3:V eq5 R6 F4:S
+S5 F5:S bk3:S sr2 L15 sr3 I2:G oq1 sw1 T14 xt9:T xc9:S N12:G L16 bt4 T15
+N13:G et12 bt5 et13 M14 M15 bk4:S X14 X15 eg12 eg13 S6 xq9 I5:V eq6 R7
+F6:S S7 F7:S bk5:S sr4 L17 sr5 I4:G oq2 sw2 T16 xt10:T xc10:S N14:G L18 bt6
+T17 N15:G et14 bt7 et15 M16 M17 bk6:S X16 X17 eg14 eg15 S8 xq10 I7:V eq7
+R8 F8:S S9 F9:S bk7:S sr6 L19 sr7 I6:G oq3 sw3 T18 xt11:T xc11:S N16:G L20
+bt8 T19 N17:G et16 bt9 et17 M18 M19 bk8:S X18 X19 eg16 eg17 S10 xq11 I9:V
+eq8 R9 F10:S S11 F11:S bk9:S sr8 L21 sr9 I8:G oq4 sw4 T20 xt12:T xc12:S N18:G
+L22 bt10 T21 N19:G et18 bt11 et19 M20 M21 bk10:S X20 X21 eg18 eg19 S12 xq12
+I11:V eq9 R10 F12:S S13 F13:S bk11:S sr10 L23 sr11 I10:G oq5 sw5 T22 xt13:T xc13:S
+N20:G L24 bt12 T23 N21:G et20 bt13 et21 M22 M23 bk12:S X22 X23 eg20 eg21 S14
+xq13 I13:V eq10 R11 F14:S S15 F15:S bk13:S sr12 L25 sr13 I12:G oq6 sw6 T24 xt14:T
+xc14:S N22:G L26 bt14 T25 N23:G et22 bt15 et23 M24 M25 bk14:S X24 X25 eg22 eg23
+S16 xq14 I15:V eq11 R12 F16:S S17 F17:S bk15:S sr14 L27 sr15 I14:G oq7 sw7 L29
+T26 N24:G M26 T27 S19 X26 F19:S N25:G et24 xt15:W et25 L28 bt17 eg24 M27 xc15:S
+X27 S18 eg25 xq15 I17:G I16:G eq12 R13 oq8 bt16 L30 L31 bk17:S F18:S N26:G bt18
+et26 bt19 T28 T29 N27:G M28 M29 bk16:S bk18:S X29 X28 et27 I18:G eg26 eg27 S20
+S21 I19:V eq13 R14 oq9 F21:V T30 T31 M30 N29:G N28:G S22 F20:S bk19:S S23 bt20
+S24 F22:S et29 et28 bt21 bk20:S F23:S S25 X30 M31 X31 bt23 S27 bt22 I20:G eg28
+eg29 R15 I21:V N31:V N30:V F24:S bk23:S F25:S sr16 sr17 sr18 sr19 sw9 sr20 sw8 oq10
+bk21:S bk22:S sw10 sr21 sr23 sr22 I22:G F27:V et31 et30 eg31 eg30 eq14 S26 bt24 bt25
+F26:S bt26 I24:G bk24:S bk26:S eq15 I23:V S28 S29 bk25:S I25:V oq11 I26:V I27:V oq13 F29:V
+F28:S sr24 ss0 sw11 sr26 sr25 bt27 S30 bk27:S oq12 I28:V I29:V oq14 F30:S bt28 bk28:S
+sr27 sw13 sw12 sr28 sw14 S31 bt29 F31:S bk29:V sr29 bt30 bk30:S sr30 bt31 bk31:S sr31
+I31:V I30:V oq15 ss1 sw15
 """
 LOADS = "k0a x0 k0b k1 x1 v0 q00 x2 v1 q10 x3 q01 q11 c"
 
@@ -121,6 +123,8 @@ def tile_softproductquantasymmetricscores_x1_kernel(tc, x, q, key, val, nrm, gai
         for u in range(len(done), UNITS):
             load_x(u)
 
+        zeros = keep.tile([P, C], BF16, name="zeros")
+        nc.vector.memset(zeros[:], 0.0)
         ident = keep.tile([P, P], F32, name="ident")
         make_identity(nc, ident[:])
         ident_bf = keep.tile([P, P], BF16, name="ident_bf")
@@ -142,7 +146,7 @@ def tile_softproductquantasymmetricscores_x1_kernel(tc, x, q, key, val, nrm, gai
         x_mx = {}
         e_mx = [mx_tiles("e%d" % u, PAIR) for u in range(UNITS)]
         out_codes = keep.tile([P, 2, N], U32, name="out_codes", align_bytes=64)
-        out_scales = keep.tile([P, 2, N], U8, name="out_scales", align_bytes=64)
+        out_scales = [keep.tile([P, 2, w], U8, name="out_scales%d" % w, align_bytes=64) for w in (1536, 512)]
 
         def quantise(codes, scales, grouped):
             nc.vector.quantize_mx(out=codes.bitcast(FP8X4), scales=scales, in_=grouped[:].rearrange("p n t -> p (n t)"))
@@ -171,6 +175,8 @@ def tile_softproductquantasymmetricscores_x1_kernel(tc, x, q, key, val, nrm, gai
         def turn(eng, name, src):
             turned = bank(name, [P, 2, 2, P])
             st[name] = turned
+            if eng != "T":
+                nc.tensor.matmul(turned[:].rearrange("p a u r -> p (a u r)"), lhsT=ident_bf[:], rhs=src[:, 0, :], start=True, stop=True)
             for a in range(2):
                 words = src[:, a, :].bitcast(F32)
                 for u in range(2):
@@ -190,11 +196,15 @@ def tile_softproductquantasymmetricscores_x1_kernel(tc, x, q, key, val, nrm, gai
             x_mx[u] = (x_codes, x_scales)
             quantise(x_codes[:], x_scales[:], grouped(("x", u)))
 
-        def warm_up(eng):
-            wb = bank("warm", [P, C])
-            for i in range(WARM):
+        def warm_up(eng, i):
+            if eng != "T":
+                wb = bank(("warm", i), [P, C])
                 nc.tensor.matmul(wb[:], lhsT=ident_bf[:], rhs=zeros[:], start=True, stop=True)
-            release("warm")
+                release(("warm", i))
+            else:
+                n = free_banks[0]
+                free_banks.remove(n)
+                free_banks.append(n)
 
         def nrm_spread(eng, g):
             nb = bank(("nb", g), [P, 4, P])
@@ -282,8 +292,9 @@ def tile_softproductquantasymmetricscores_x1_kernel(tc, x, q, key, val, nrm, gai
             release(("s", v, b))
 
         def interleave(eng, v, a):
-            src = st["pf", v][:, :, P * a : P * (a + 1)].rearrange("p t n -> p n t")
-            dst = grouped(("o", v))[:, P * a : P * (a + 1), :]
+            cols = slice(0, SPLIT) if a == 0 else slice(SPLIT, PAIR)
+            src = st["pf", v][:, :, cols].rearrange("p t n -> p n t")
+            dst = grouped(("o", v))[:, cols, :]
             if eng == "V":
                 nc.vector.tensor_copy(out=dst, in_=src)
             else:
@@ -298,7 +309,7 @@ def tile_softproductquantasymmetricscores_x1_kernel(tc, x, q, key, val, nrm, gai
             cols = slice(0, 1536) if part == 0 else slice(1536, N)
             for quad in range(4):
                 nc.sync.dma_start(out=out_2[:, 4 * quad : 4 * quad + 4, cols].rearrange("h r n -> r h n").bitcast(I32),
-                                  in_=out_scales[32 * quad : 32 * quad + 4, :, cols].bitcast(I32))
+                                  in_=out_scales[part][32 * quad : 32 * quad + 4, :, :].bitcast(I32))
 
         def back_turn(eng, v, a):
             bb = bank(("b", v, a), [P, 4, P])
@@ -320,9 +331,8 @@ def tile_softproductquantasymmetricscores_x1_kernel(tc, x, q, key, val, nrm, gai
             tasks[name] = (fn, args)
 
         if WARM:
-            zeros = keep.tile([P, C], BF16, name="zeros")
-            nc.vector.memset(zeros[:], 0.0)
-            add("W", warm_up)
+            for i in range(WARM):
+                add("w%d" % i, warm_up, i)
         for g in range(G):
             add("nt%d" % g, nrm_spread, g)
             add("nc%d" % g, nrm_copy, g)
@@ -368,7 +378,7 @@ def tile_softproductquantasymmetricscores_x1_kernel(tc, x, q, key, val, nrm, gai
                 add("sr%d" % (2 * v + a), store_rows, v, a)
             for a in range(2):
                 add("I%d" % (2 * v + a), interleave, v, a)
-            add("oq%d" % v, quant, ("o", v), out_codes[:, h, cols], out_scales[:, h, cols])
+            add("oq%d" % v, quant, ("o", v), out_codes[:, h, cols], out_scales[j // 6][:, h, PAIR * (j % 6) : PAIR * (j % 6 + 1)])
             add("sw%d" % v, store_words, v)
             if v in (11, 15):
                 add("ss%d" % (v // 12), store_scales, v // 12)

from contextlib import ExitStack

import concourse.mybir as mybir
from concourse.masks import make_identity

N, Q, G, D, C = 2048, 1024, 2, 512, 512
FLOPS = 2 * G * N * D * C + 2 * G * Q * D * C + 2 * N * Q * G * C

F32 = mybir.dt.float32
BF16 = mybir.dt.bfloat16
U32 = mybir.dt.uint32
I32 = mybir.dt.int32
U8 = mybir.dt.uint8
FP8X4 = mybir.dt.float8_e4m3fn_x4
ALU = mybir.AluOpType
ACT = mybir.ActivationFunctionType

P = 128
PAIR = 256
UNITS = 16
WARM = 6
SPLIT = 192
ORDER = """
w1:W w2:W w4:W kt0:T w5:W nt1 xt0:T nt0 kt3:T w0:T w3:T kt1:T xt1:W kc1:S kc0:V kq0
xc0:V xq0 kc3:V kq3 kq1 nc0:V kt4:T kc4:S kt2:W kc2:S xc1:S kq2 kq4 kt5:W kt6:T L1
L0 kt7:T kt8:T kc5:S kc6:S kc7:S kt9:W xq1 T1 T0 M1 kq7 M0 kq6 kc8:V kq5
xt2:W kt10:W kc9:S kq9 kq8 xc2:V X1 X0 kc10:S kq10 xq2 R0 nc1:S xt3:T kt11:W kc11:S
xc3:S L3 L2 kt13:T kc13:S kt14:W kt12:W T3 T2 M3 N0:G N1:G et0 et1 xt4:T kt15:T
xq3 M2 bc kq11 kq13 eg0 X3 X2 kc14:S kc12:S eg1 kq14 eq0 R1 kq12 L5
xc4:S kc15:S lm1 L4 lm0 lc1:S lm4 lm2 N3:G N2:G L7 xt5:T et2 lc0:S lc2:S T5
T4 M5 M4 kq15 xq4 eg2 lq0 X5 X4 R2 xc5:S lc4:S et3 eg3 lm7 L6
T6 lc7:S T7 N5:G N4:G M6 lm10 lm6 lm3 lm5 lc6:S lc5:S lq3 M7 lq2 lm8
lm14 lc3:S lc8:S lm9 et4 et5 lm15 eg4 lq1 eg5 eq1 X6 X7 R3 L9 L8
xt6:T lc9:S lm11 lc14:S xc6:S lm13 lc10:S lc13:S lc15:S lc11:S xq5 T9 T8 N6:V eq2 M9
M8 lq4 N7:G S1 X9 X8 et6 L11 lm12 et7 eg6 lq7 lq5 eg7 S0 L10
lc12:S xq6 eq3 R4 lq6 F1:S F0:S L12 xt7:W N8:G T11 T10 M11 et8 eg8 M10
N9:G bt0 et9 xc7:S X11 eg9 xq7 L13 S2 bk0:S X10 F2:S S3 F3:S I1:G I0:G
oq0 eq4 sr0 bt1 sw0 bk1:S sr1 R5 T12 xt8:T xc8:S N10:G L14 bt2 T13 N11:G
et10 bt3 et11 M12 M13 bk2:S X12 X13 eg10 eg11 S4 xq8 I3:V eq5 R6 F4:S
S5 F5:S bk3:S sr2 L15 sr3 I2:G oq1 sw1 T14 xt9:T xc9:S N12:G L16 bt4 T15
N13:G et12 bt5 et13 M14 M15 bk4:S X14 X15 eg12 eg13 S6 xq9 I5:V eq6 R7
F6:S S7 F7:S bk5:S sr4 L17 sr5 I4:G oq2 sw2 T16 xt10:T xc10:S N14:G L18 bt6
T17 N15:G et14 bt7 et15 M16 M17 bk6:S X16 X17 eg14 eg15 S8 xq10 I7:V eq7
R8 F8:S S9 F9:S bk7:S sr6 L19 sr7 I6:G oq3 sw3 T18 xt11:T xc11:S N16:G L20
bt8 T19 N17:G et16 bt9 et17 M18 M19 bk8:S X18 X19 eg16 eg17 S10 xq11 I9:V
eq8 R9 F10:S S11 F11:S bk9:S sr8 L21 sr9 I8:G oq4 sw4 T20 xt12:T xc12:S N18:G
L22 bt10 T21 N19:G et18 bt11 et19 M20 M21 bk10:S X20 X21 eg18 eg19 S12 xq12
I11:V eq9 R10 F12:S S13 F13:S bk11:S sr10 L23 sr11 I10:G oq5 sw5 T22 xt13:T xc13:S
N20:G L24 bt12 T23 N21:G et20 bt13 et21 M22 M23 bk12:S X22 X23 eg20 eg21 S14
xq13 I13:V eq10 R11 F14:S S15 F15:S bk13:S sr12 L25 sr13 I12:G oq6 sw6 T24 xt14:T
xc14:S N22:G L26 bt14 T25 N23:G et22 bt15 et23 M24 M25 bk14:S X24 X25 eg22 eg23
S16 xq14 I15:V eq11 R12 F16:S S17 F17:S bk15:S sr14 L27 sr15 I14:G oq7 sw7 L29
T26 N24:G M26 T27 S19 X26 F19:S N25:G et24 xt15:W et25 L28 bt17 eg24 M27 xc15:S
X27 S18 eg25 xq15 I17:G I16:G eq12 R13 oq8 bt16 L30 L31 bk17:S F18:S N26:G bt18
et26 bt19 T28 T29 N27:G M28 M29 bk16:S bk18:S X29 X28 et27 I18:G eg26 eg27 S20
S21 I19:V eq13 R14 oq9 F21:V T30 T31 M30 N29:G N28:G S22 F20:S bk19:S S23 bt20
S24 F22:S et29 et28 bt21 bk20:S F23:S S25 X30 M31 X31 bt23 S27 bt22 I20:G eg28
eg29 R15 I21:V N31:V N30:V F24:S bk23:S F25:S sr16 sr17 sr18 sr19 sw9 sr20 sw8 oq10
bk21:S bk22:S sw10 sr21 sr23 sr22 I22:G F27:V et31 et30 eg31 eg30 eq14 S26 bt24 bt25
F26:S bt26 I24:G bk24:S bk26:S eq15 I23:V S28 S29 bk25:S I25:V oq11 I26:V I27:V oq13 F29:V
F28:S sr24 ss0 sw11 sr26 sr25 bt27 S30 bk27:S oq12 I28:V I29:V oq14 F30:S bt28 bk28:S
sr27 sw13 sw12 sr28 sw14 S31 bt29 F31:S bk29:V sr29 bt30 bk30:S sr30 bt31 bk31:S sr31
I31:V I30:V oq15 ss1 sw15
"""
LOADS = "k0a x0 k0b k1 x1 v0 q00 x2 v1 q10 x3 q01 q11 c"


def tile_softproductquantasymmetricscores_x1_kernel(tc, x, q, key, val, nrm, gain, base, out_0, out_1, out_2):
    nc = tc.nc
    with ExitStack() as ctx:
        keep = ctx.enter_context(tc.tile_pool(name="keep", bufs=1))
        work = ctx.enter_context(tc.tile_pool(name="work", bufs=3))
        psum = ctx.enter_context(tc.psum_pool(name="psum", bufs=1))
        ctx.enter_context(tc.manual_schedule())

        free_banks = list(range(8))
        held = {}

        def bank(name, shape):
            n = free_banks[0]
            free_banks.remove(n)
            held[name] = n
            return psum.tile(shape, F32, name="bank%d" % n, tag="bank%d" % n)

        def release(name):
            free_banks.append(held[name])

        key_sb = [keep.tile([P, 4, D], BF16, name="key_sb%d" % g) for g in range(G)]
        val_sb = [keep.tile([P, 4, D], BF16, name="val_sb%d" % g) for g in range(G)]
        q_sb = [[keep.tile([P, 4, D], BF16, name="q_sb%d%d" % (g, h)) for h in range(2)] for g in range(G)]
        x_sb = [keep.tile([P, 2, D], BF16, name="x_sb%d" % u) for u in range(UNITS)]
        nrm_col = keep.tile([P, G, 4], BF16, name="nrm_col")
        gain_col = keep.tile([P, G, 4], BF16, name="gain_col")
        base_col = keep.tile([P, 2, 4], BF16, name="base_col")

        def load_book(dst, rows):
            nc.sync.dma_start(out=dst, in_=rows.rearrange("(m t) k -> m t k", t=4))

        def load_x(u):
            j, g = divmod(u, G)
            nc.sync.dma_start(out=x_sb[u][:], in_=x[g, PAIR * j : PAIR * (j + 1), :].rearrange("(a p) k -> p a k", a=2))

        key0 = key[0].rearrange("(m t) k -> m t k", t=4)
        nc.scalar.dma_start(out=nrm_col[:], in_=nrm.rearrange("g (m t) -> m g t", t=4))
        done = []
        for w in LOADS.split():
            if w == "k0a":
                nc.sync.dma_start(out=key_sb[0][:, 0:2, :], in_=key0[:, 0:2, :])
            elif w == "k0b":
                nc.sync.dma_start(out=key_sb[0][:, 2:4, :], in_=key0[:, 2:4, :])
            elif w == "k1":
                load_book(key_sb[1][:], key[1])
            elif w == "c":
                nc.sync.dma_start(out=gain_col[:], in_=gain.rearrange("g (m t) -> m g t", t=4))
                nc.sync.dma_start(out=base_col[:], in_=base.rearrange("(h m t) -> m h t", h=2, t=4))
            elif w[0] == "x":
                load_x(len(done))
                done.append(w)
            elif w[0] == "v":
                load_book(val_sb[int(w[1])][:], val[int(w[1])])
            else:
                load_book(q_sb[int(w[1])][int(w[2])][:], q[int(w[1]), 512 * int(w[2]) : 512 * (int(w[2]) + 1), :])
        for u in range(len(done), UNITS):
            load_x(u)

        zeros = keep.tile([P, C], BF16, name="zeros")
        nc.vector.memset(zeros[:], 0.0)
        ident = keep.tile([P, P], F32, name="ident")
        make_identity(nc, ident[:])
        ident_bf = keep.tile([P, P], BF16, name="ident_bf")
        nc.vector.tensor_copy(out=ident_bf[:], in_=ident[:])
        warm = keep.tile([P, 1], F32, name="warm")
        nc.scalar.activation(out=warm[:], in_=ident[:, 0:1], func=ACT.Exp)

        nrm_bc = keep.tile([P, G, C], F32, name="nrm_bc")
        base_f = keep.tile([P, 2, 4], F32, name="base_f")

        def mx_tiles(name, width):
            return (keep.tile([P, width], U32, name=name + "_codes", align_bytes=64),
                    keep.tile([P, width], U8, name=name + "_scales", align_bytes=64))

        key_mx = [mx_tiles("key%d" % g, C) for g in range(G)]
        val_mx = [mx_tiles("val%d" % g, C) for g in range(G)]
        q_mx = [mx_tiles("q%d" % g, Q) for g in range(G)]
        lut_mx = [mx_tiles("lut%d" % g, Q) for g in range(G)]
        x_mx = {}
        e_mx = [mx_tiles("e%d" % u, PAIR) for u in range(UNITS)]
        out_codes = keep.tile([P, 2, N], U32, name="out_codes", align_bytes=64)
        out_scales = [keep.tile([P, 2, w], U8, name="out_scales%d" % w, align_bytes=64) for w in (1536, 512)]

        def quantise(codes, scales, grouped):
            nc.vector.quantize_mx(out=codes.bitcast(FP8X4), scales=scales, in_=grouped[:].rearrange("p n t -> p (n t)"))

        def mx(out, lhs, lcols, rhs, rcols, start, stop):
            nc.tensor.matmul_mx(out=out, lhsT=lhs[0][:, lcols].bitcast(FP8X4), lhsT_scale=lhs[1][:, lcols],
                                rhs=rhs[0][:, rcols].bitcast(FP8X4), rhs_scale=rhs[1][:, rcols], start=start, stop=stop)

        st = {}
        tasks = {}

        def evac(dst, src, eng):
            if eng == "V":
                nc.vector.tensor_copy(out=dst, in_=src)
            else:
                nc.scalar.copy(out=dst, in_=src)

        def shared(name, tag, shape, dtype, bufs):
            if name not in st:
                st[name] = work.tile(shape, dtype, name=tag, tag=tag, bufs=bufs, align_bytes=64)
            return st[name]

        def grouped(name):
            return shared(("grp", name), "grouped", [P, PAIR, 4], BF16, 10)

        def turn(eng, name, src):
            turned = bank(name, [P, 2, 2, P])
            st[name] = turned
            if eng != "T":
                nc.tensor.matmul(turned[:].rearrange("p a u r -> p (a u r)"), lhsT=ident_bf[:], rhs=src[:, 0, :], start=True, stop=True)
            for a in range(2):
                words = src[:, a, :].bitcast(F32)
                for u in range(2):
                    nc.tensor.transpose(turned[:, a, u, :], words[:, u : D // 2 : 2], ident[:])

        def regroup(eng, name):
            dst = grouped(name)[:].rearrange("p n t -> p (n t)").bitcast(F32).rearrange("p (a r u) -> p a r u", a=2, u=2)
            evac(dst, st[name][:].rearrange("p a u r -> p a r u"), eng)
            release(name)

        def quant(eng, name, codes, scales):
            quantise(codes, scales, grouped(name))

        def quant_x(eng, u):
            x_codes = work.tile([P, PAIR], U32, name="x_codes", align_bytes=64, bufs=4)
            x_scales = work.tile([P, PAIR], U8, name="x_scales", align_bytes=64, bufs=4)
            x_mx[u] = (x_codes, x_scales)
            quantise(x_codes[:], x_scales[:], grouped(("x", u)))

        def warm_up(eng, i):
            if eng != "T":
                wb = bank(("warm", i), [P, C])
                nc.tensor.matmul(wb[:], lhsT=ident_bf[:], rhs=zeros[:], start=True, stop=True)
                release(("warm", i))
            else:
                n = free_banks[0]
                free_banks.remove(n)
                free_banks.append(n)

        def nrm_spread(eng, g):
            nb = bank(("nb", g), [P, 4, P])
            st["nb", g] = nb
            for t in range(4):
                nc.tensor.matmul(nb[:, t, :], lhsT=nrm_col[:, g, t : t + 1].to_broadcast([P, P]), rhs=ident_bf[:], start=True, stop=True)

        def nrm_copy(eng, g):
            evac(nrm_bc[:, g, :], st["nb", g][:].rearrange("p t n -> p (t n)"), eng)
            release(("nb", g))

        def base_cast(eng):
            nc.vector.tensor_copy(out=base_f[:], in_=base_col[:])

        def lut_matmuls(eng, g, col):
            lb = bank(("lut", g, col), [P, 4, P])
            st["lut", g, col] = lb
            for t in range(4):
                mx(lb[:, t, :], val_mx[g], slice(P * t, P * (t + 1)), q_mx[g], slice(col, col + P), True, True)

        def lut_copy(eng, g, col):
            off = col % PAIR
            evac(grouped(("lut", g, col - off))[:, off : off + P, :], st["lut", g, col][:].rearrange("p t n -> p n t"), eng)
            release(("lut", g, col))

        def logits(eng, u, a):
            lb = bank(("l", u, a), [P, C])
            st["l", u, a] = lb
            mx(lb[:], x_mx[u], slice(P * a, P * (a + 1)), key_mx[u % G], slice(0, C), True, True)

        def offsets(eng, u, a):
            neg = shared(("neg", u), "neg", [P, 2, C], F32, 3)
            nc.vector.tensor_tensor(out=neg[:, a, :], in0=nrm_bc[:, u % G, :], in1=st["l", u, a][:], op=ALU.subtract)
            release(("l", u, a))

        def minimum(eng, u, a):
            mn = shared(("mn", u), "mn", [P, 2], F32, 4)
            nc.vector.tensor_reduce(out=mn[:, a : a + 1], in_=st["neg", u][:, a, :], axis=mybir.AxisListType.X, op=ALU.min)

        def expo(eng, u, a):
            w = shared(("w", u), "w", [P, 2, C], F32, 3)
            sm = shared(("sm", u), "sm", [P, 2], F32, 4)
            nc.scalar.activation(out=w[:, a, :], in_=st["neg", u][:, a, :], func=ACT.Exp, scale=-1.0, bias=st["mn", u][:, a : a + 1],
                                 accum_out=sm[:, a : a + 1])

        def recip(eng, u):
            rc = shared(("rc", u), "rc", [P, 2], F32, 4)
            nc.vector.reciprocal(out=rc[:], in_=st["sm", u][:])

        def normalise(eng, u, a):
            un = shared(("un", u, a), "un", [P, C], F32, 4)
            e = nc.vector if eng == "V" else nc.gpsimd
            e.tensor_scalar(out=un[:], in0=st["w", u][:, a, :], scalar1=st["rc", u][:, a : a + 1], scalar2=float(C), op0=ALU.mult, op1=ALU.mult)

        def e_turn(eng, u, a):
            eb = bank(("et", u, a), [P, 4, P])
            st["et", u, a] = eb
            for t in range(4):
                nc.tensor.transpose(eb[:, t, :], st["un", u, a][:, P * t : P * (t + 1)], ident[:])

        def e_gain(eng, u, a):
            nc.vector.scalar_tensor_tensor(
                out=grouped(("e", u))[:, P * a : P * (a + 1), :], in0=st["et", u, a][:].rearrange("p t n -> p n t"), scalar=1.0,
                in1=gain_col[:, u % G, :].unsqueeze(1).to_broadcast([P, P, 4]), op0=ALU.subtract, op1=ALU.mult)
            release(("et", u, a))

        def scores(eng, v, b):
            j, h = divmod(v, 2)
            sb = bank(("s", v, b), [P, 2, PAIR])
            st["s", v, b] = sb
            for tt in range(2):
                t = 2 * b + tt
                for g in range(G):
                    mx(sb[:, tt, :], lut_mx[g], slice(512 * h + P * t, 512 * h + P * (t + 1)), e_mx[G * j + g], slice(0, PAIR), g == 0, g == G - 1)

        def finish(eng, v, b):
            h = v % 2
            pf = shared(("pf", v), "pf", [P, 4, PAIR], F32, 3)
            for t in (2 * b, 2 * b + 1):
                src = st["s", v, b][:, t % 2, :]
                if eng == "V":
                    nc.vector.tensor_scalar(out=pf[:, t, :], in0=src, scalar1=1.0 / 32.0, scalar2=base_f[:, h, t : t + 1], op0=ALU.mult, op1=ALU.add)
                else:
                    nc.scalar.activation(out=pf[:, t, :], in_=src, func=ACT.Identity, scale=1.0 / 32.0, bias=base_f[:, h, t : t + 1])
            release(("s", v, b))

        def interleave(eng, v, a):
            cols = slice(0, SPLIT) if a == 0 else slice(SPLIT, PAIR)
            src = st["pf", v][:, :, cols].rearrange("p t n -> p n t")
            dst = grouped(("o", v))[:, cols, :]
            if eng == "V":
                nc.vector.tensor_copy(out=dst, in_=src)
            else:
                nc.gpsimd.tensor_scalar(out=dst, in0=src, scalar1=1.0, scalar2=1.0, op0=ALU.mult, op1=ALU.mult)

        def store_words(eng, v):
            j, h = divmod(v, 2)
            cols = slice(PAIR * j, PAIR * (j + 1))
            nc.sync.dma_start(out=out_1[h, :, cols, :].rearrange("p n t -> p (n t)").bitcast(I32), in_=out_codes[:, h, cols].bitcast(I32))

        def store_scales(eng, part):
            cols = slice(0, 1536) if part == 0 else slice(1536, N)
            for quad in range(4):
                nc.sync.dma_start(out=out_2[:, 4 * quad : 4 * quad + 4, cols].rearrange("h r n -> r h n").bitcast(I32),
                                  in_=out_scales[part][32 * quad : 32 * quad + 4, :, :].bitcast(I32))

        def back_turn(eng, v, a):
            bb = bank(("b", v, a), [P, 4, P])
            st["b", v, a] = bb
            for t in range(4):
                nc.tensor.transpose(bb[:, t, :], st["pf", v][:, t, P * a : P * (a + 1)], ident[:])

        def back_copy(eng, v, a):
            res = shared(("res", v, a), "res", [P, 512], F32, 6)
            evac(res[:].rearrange("r (m t) -> r m t", t=4), st["b", v, a][:].rearrange("r t m -> r m t"), eng)
            release(("b", v, a))

        def store_rows(eng, v, a):
            j, h = divmod(v, 2)
            rows = slice(PAIR * j + P * a, PAIR * j + P * (a + 1))
            nc.sync.dma_start(out=out_0[rows, 512 * h : 512 * (h + 1)], in_=st["res", v, a][:])

        def add(name, fn, *args):
            tasks[name] = (fn, args)

        if WARM:
            for i in range(WARM):
                add("w%d" % i, warm_up, i)
        for g in range(G):
            add("nt%d" % g, nrm_spread, g)
            add("nc%d" % g, nrm_copy, g)
        add("bc", base_cast)
        i = 0
        for src, dst, col in ([(key_sb[0], key_mx[0], 0), (key_sb[1], key_mx[1], 0), (val_sb[0], val_mx[0], 0), (q_sb[0][0], q_mx[0], 0),
                               (val_sb[1], val_mx[1], 0), (q_sb[1][0], q_mx[1], 0), (q_sb[0][1], q_mx[0], 512), (q_sb[1][1], q_mx[1], 512)]):
            for hh in range(2):
                cols = slice(col + PAIR * hh, col + PAIR * (hh + 1))
                add("kt%d" % i, turn, ("book", i), src[:, 2 * hh : 2 * hh + 2, :])
                add("kc%d" % i, regroup, ("book", i))
                add("kq%d" % i, quant, ("book", i), dst[0][:, cols], dst[1][:, cols])
                i += 1
        for i, (g, col) in enumerate([(0, 0), (0, 256), (1, 0), (1, 256), (0, 512), (0, 768), (1, 512), (1, 768)]):
            for b in range(2):
                add("lm%d" % (2 * i + b), lut_matmuls, g, col + P * b)
                add("lc%d" % (2 * i + b), lut_copy, g, col + P * b)
            add("lq%d" % i, quant, ("lut", g, col), lut_mx[g][0][:, col : col + PAIR], lut_mx[g][1][:, col : col + PAIR])
        for u in range(UNITS):
            add("xt%d" % u, turn, ("x", u), x_sb[u])
            add("xc%d" % u, regroup, ("x", u))
            add("xq%d" % u, quant_x, u)
            for a in range(2):
                add("L%d" % (2 * u + a), logits, u, a)
                add("T%d" % (2 * u + a), offsets, u, a)
                add("M%d" % (2 * u + a), minimum, u, a)
                add("X%d" % (2 * u + a), expo, u, a)
            add("R%d" % u, recip, u)
            for a in range(2):
                add("N%d" % (2 * u + a), normalise, u, a)
                add("et%d" % (2 * u + a), e_turn, u, a)
                add("eg%d" % (2 * u + a), e_gain, u, a)
            add("eq%d" % u, quant, ("e", u), e_mx[u][0][:], e_mx[u][1][:])
        for v in range(UNITS):
            j, h = divmod(v, 2)
            cols = slice(PAIR * j, PAIR * (j + 1))
            for b in range(2):
                add("S%d" % (2 * v + b), scores, v, b)
                add("F%d" % (2 * v + b), finish, v, b)
            for a in range(2):
                add("bt%d" % (2 * v + a), back_turn, v, a)
                add("bk%d" % (2 * v + a), back_copy, v, a)
                add("sr%d" % (2 * v + a), store_rows, v, a)
            for a in range(2):
                add("I%d" % (2 * v + a), interleave, v, a)
            add("oq%d" % v, quant, ("o", v), out_codes[:, h, cols], out_scales[j // 6][:, h, PAIR * (j % 6) : PAIR * (j % 6 + 1)])
            add("sw%d" % v, store_words, v)
            if v in (11, 15):
                add("ss%d" % (v // 12), store_scales, v // 12)
        for word in ORDER.split() or list(tasks):
            name, eng = (word + ":").split(":")[:2]
            tasks[name][0](eng, *tasks[name][1])
